import numpy as np
import ml_dtypes


def mxq(x, axis, fmt="e4m3"):
    dtype, down = {"e4m3": (ml_dtypes.float8_e4m3fn, 7), "e5m2": (ml_dtypes.float8_e5m2, 14)}[fmt]
    v = np.moveaxis(np.asarray(x, np.float32).astype(ml_dtypes.bfloat16).astype(np.float64), axis, -1)
    blocks = v.reshape(v.shape[:-1] + (-1, 32))
    amax = np.abs(blocks).max(-1, keepdims=True)
    byte = np.maximum(np.where(amax > 0, np.frexp(amax)[1] - 1 + 127, 0) - down, 1)
    scale = np.exp2(byte - 127.0)
    codes = (blocks / scale).astype(np.float32).astype(dtype).astype(np.float64)
    return np.moveaxis((codes * scale).reshape(v.shape), -1, axis)


WIDE = False


def mx_kscale(k):
    if not WIDE:
        return np.ones(k)
    levels = np.array([10, -10, 5, -5, 0])
    if k % 512:
        return np.exp2(np.random.permutation(np.resize(levels, k // 32))).repeat(32)
    a = np.empty((k // 512, 16))
    for p in range(k // 512):
        a[p, :8] = np.random.permutation(np.resize(levels, 8))
        for g in range(8):
            far = levels[np.abs(levels - a[p, g]) >= 10]
            a[p, g + 8] = far[np.random.randint(len(far))]
    return np.exp2(a.ravel()).repeat(32)


def f64(x):
    return np.asarray(x).astype(np.float64)


def striped8(idx):
    return np.asarray(idx).reshape(8, -1, 16).transpose(0, 2, 1).reshape(128, -1).astype(np.uint16)


def unstriped8(offs):
    return offs.reshape(8, 16, -1).transpose(0, 2, 1).reshape(8, -1).astype(np.int64)


def pick8(x, idx, run):
    r = np.arange(len(x))
    return x[r[:, None], idx[r % (8 * run) // run]]


E2M1 = np.array([0.0, 0.5, 1.0, 1.5, 2.0, 3.0, 4.0, 6.0, -0.0, -0.5, -1.0, -1.5, -2.0, -3.0, -4.0, -6.0])


def pack_weight(w, fmt):
    k, n = w.shape
    w = f64(np.asarray(w, np.float32).astype(ml_dtypes.bfloat16)).reshape(k // 32, 32, n)
    amax = np.abs(w).max(1)
    if fmt == "e4m3":
        byte = np.frexp(amax)[1] - 1 + 127 - 7
    else:
        mant, ex = np.frexp(amax / 6.0)
        byte = np.where(mant > 0.5, ex, ex - 1) + 127
    byte = np.clip(np.where(amax > 0, byte, 1), 1, 254)
    scaled = (w * np.exp2(127.0 - byte)[:, None, :]).reshape(k, n).astype(np.float32)
    by_word = np.ascontiguousarray(scaled.reshape(k // 512, 128, 4, n).transpose(0, 1, 3, 2))
    if fmt == "e4m3":
        words = by_word.astype(ml_dtypes.float8_e4m3fn).view(np.uint8)
    else:
        c = by_word.astype(ml_dtypes.float4_e2m1fn).view(np.uint8) & 0xF
        words = (c[..., 0::2] | (c[..., 1::2] << 4)).reshape(k // 512, 128, 2 * n)
    return np.ascontiguousarray(words), np.ascontiguousarray(byte.astype(np.uint8).reshape(k // 512, 16, n))


def unpack_weight(words, scales, fmt):
    g, _, n = scales.shape
    words = np.ascontiguousarray(words).reshape(g, 128, n, -1)
    if fmt == "e4m3":
        vals = words.view(ml_dtypes.float8_e4m3fn).astype(np.float64)
    else:
        nib = np.empty((g, 128, n, 4), np.uint8)
        nib[..., 0::2] = words & 0xF
        nib[..., 1::2] = words >> 4
        vals = E2M1[nib]
    vals = vals * np.repeat(np.exp2(scales.astype(np.float64) - 127.0), 8, axis=1)[..., None]
    return vals.transpose(0, 1, 3, 2).reshape(g * 512, n)


def softplus(v):
    return np.log(1.0 + np.exp(v))


D, T, I, Q = 512, 1024, 512, 128


def setup_inputs():
    n = np.random.standard_normal
    idx = np.stack([np.random.permutation(T)[:I] for _ in range(8)])
    idx2 = np.stack([np.random.permutation(T)[:I] for _ in range(8)])
    idx3 = np.stack([np.random.permutation(T)[:I] for _ in range(8)])
    fd = mx_kscale(D)
    keysp = pack_weight(n((D, T)) / fd[:, None], "e2m1")
    return {
        "query": (n((D, Q)) * 0.9 / np.sqrt(D) * fd[:, None]).astype(np.float32),
        "query2": (n((D, Q)) * 0.9 / np.sqrt(D) * fd[:, None]).astype(np.float32),
        "keys_words": keysp[0],
        "keys_scales": keysp[1],
        "lam": (np.random.uniform(0.6, 1.2, (Q, 1))).astype(np.float32),
        "old": (1.0 * n((Q, T))).astype(np.float32),
        "offs": striped8(idx),
        "offs2": striped8(idx2),
        "offs3": striped8(idx3),
    }


def reference(query, query2, keys_words, keys_scales, lam, old, offs, offs2, offs3):
    idx = unstriped8(offs)
    idx2 = unstriped8(offs2)
    idx3 = unstriped8(offs3)
    keysu = unpack_weight(keys_words, keys_scales, "e2m1")
    queryq = mxq(f64(query), 0, "e4m3")
    a = queryq.T @ keysu
    query2q = mxq(f64(query2), 0, "e4m3")
    b = query2q.T @ keysu
    w = pick8(a, idx, 16) / (softplus(pick8(b, idx2, 16)) + 0.5) * f64(lam)
    f1 = np.zeros((Q, T))
    f1[np.arange(Q)[:, None], idx[np.arange(Q) % 128 // 16]] = w
    f2 = f1 + f64(old)
    y = pick8(f2, idx3, 16) * w
    return y

@@ -1,0 +1,145 @@
+from contextlib import ExitStack
+
+import concourse.mybir as mybir
+
+D, T, I, Q = 512, 1024, 512, 128
+FLOPS = 2 * 2 * D * T * Q
+
+F32 = mybir.dt.float32
+BF16 = mybir.dt.bfloat16
+I32 = mybir.dt.int32
+U32 = mybir.dt.uint32
+U16 = mybir.dt.uint16
+U8 = mybir.dt.uint8
+FP8X4 = mybir.dt.float8_e4m3fn_x4
+FP4X4 = mybir.dt.float4_e2m1fn_x4
+ALU = mybir.AluOpType
+ACT = mybir.ActivationFunctionType
+
+P = 128
+PACK = 4
+CAP_AT = 40.0
+LEAD = 128
+
+
+def tile_attend_worthfor_lean_throughtimes_heads_kernel(
+    tc, query, query2, keys_words, keys_scales, lam, old, offs, offs2, offs3, out
+):
+    nc = tc.nc
+    with ExitStack() as ctx:
+        sb = ctx.enter_context(tc.tile_pool(name="sb", bufs=1))
+        ps = ctx.enter_context(tc.psum_pool(name="ps", bufs=1))
+
+        key_scales = sb.tile([P, T], U8, name="key_scales", align_bytes=64)
+        key_words = sb.tile([P, 2 * T], U8, name="key_words", align_bytes=64)
+        f1 = sb.tile([P, T], F32, name="f1")
+        nc.gpsimd.memset(key_scales[:].bitcast(I32), 0)
+        nc.vector.memset(f1[:], 0.0)
+
+        cap_at = sb.tile([P, 1], F32, name="cap_at")
+        cap = sb.tile([P, 1], F32, name="cap")
+        nc.vector.memset(cap_at[:], CAP_AT)
+        raw_b = sb.tile([P, PACK, Q], F32, name="raw_b", tag="raw_b_then_old")
+        raw_a = sb.tile([P, PACK, Q], F32, name="raw_a")
+        nc.sync.dma_start(out=raw_b[:], in_=query2.rearrange("(p j) q -> p j q", j=PACK))
+        nc.sync.dma_start(out=key_words[:].bitcast(I32), in_=keys_words[0].bitcast(I32))
+        for quad in range(4):
+            nc.scalar.dma_start(
+                out=key_scales[32 * quad : 32 * quad + 4, :].bitcast(I32),
+                in_=keys_scales[0, 4 * quad : 4 * quad + 4, :].bitcast(I32),
+            )
+        nc.scalar.activation(cap[:], cap_at[:], ACT.Exp)
+        nc.sync.dma_start(out=raw_a[:], in_=query.rearrange("(p j) q -> p j q", j=PACK))
+        list_b = sb.tile([P, I // 16], U16, name="list_b")
+        list_a = sb.tile([P, I // 16], U16, name="list_a")
+        list_f = sb.tile([P, I // 16], U16, name="list_f")
+        lam_col = sb.tile([P, 1], F32, name="lam_col")
+        nc.sync.dma_start(list_b[:], offs2)
+        nc.sync.dma_start(list_a[:], offs)
+        nc.sync.dma_start(list_f[:], offs3)
+        nc.sync.dma_start(lam_col[:], lam)
+
+        def quantise(raw, tag):
+            grouped = sb.tile([P, Q, PACK], BF16, name=tag + "_grouped", align_bytes=64)
+            codes = sb.tile([P, Q], U32, name=tag + "_codes", align_bytes=64)
+            scales = sb.tile([P, Q], U8, name=tag + "_scales", align_bytes=64)
+            nc.vector.tensor_copy(
+                out=grouped[:].rearrange("p (c i) j -> p c j i", i=4),
+                in_=raw[:].rearrange("p j (c i) -> p c j i", i=4),
+            )
+            nc.vector.quantize_mx(
+                out=codes[:].bitcast(FP8X4),
+                scales=scales[:],
+                in_=grouped[:].rearrange("p q j -> p (q j)"),
+            )
+            return codes, scales
+
+        def score(codes, scales, first, width, name, tag):
+            bank = ps.tile([P, width], F32, name=name, tag=tag)
+            nc.tensor.matmul_mx(
+                out=bank[:],
+                lhsT=codes[:].bitcast(FP8X4),
+                lhsT_scale=scales[:],
+                rhs=key_words[:, 2 * first : 2 * (first + width)].bitcast(FP4X4),
+                rhs_scale=key_scales[:, first : first + width],
+                start=True,
+                stop=True,
+            )
+            return bank
+
+        b_all = sb.tile([P, T], F32, name="b_all")
+        a_all = sb.tile([P, T], F32, name="a_all")
+        codes_b, scales_b = quantise(raw_b, "b")
+        old_sb = sb.tile([P, T], F32, name="old_sb", tag="raw_b_then_old")
+        nc.sync.dma_start(old_sb[:], old)
+        for n in range(4):
+            bank = score(codes_b, scales_b, 256 * n, 256, "b%d" % n, "bank%d" % n)
+            if n % 2 == 0:
+                nc.scalar.activation(b_all[:, 256 * n : 256 * (n + 1)], bank[:], ACT.Copy)
+            else:
+                nc.vector.tensor_copy(b_all[:, 256 * n : 256 * (n + 1)], bank[:])
+        codes_a, scales_a = quantise(raw_a, "a")
+
+        exp_b = sb.tile([P, I], F32, name="exp_b")
+        picked_b = sb.tile([P, I], F32, name="picked_b")
+        capped = sb.tile([P, I], F32, name="capped")
+        log1p = sb.tile([P, I], F32, name="log1p")
+        softplus = sb.tile([P, I], F32, name="softplus")
+        half = I // 2
+        shared = sb.tile([P, I + half], F32, name="shared")
+        picked_a = shared[:, :I]
+        squared = shared[:, half:]
+        nc.scalar.activation(exp_b[:, half:], b_all[:].indirect(list_b[:, half // 16 :]), ACT.Exp)
+        nc.vector.tensor_copy(picked_b[:, :half], b_all[:].indirect(list_b[:, : half // 16]))
+        nc.scalar.activation(exp_b[:, :half], picked_b[:, :half], ACT.Exp)
+        nc.vector.tensor_copy(picked_b[:, half:], b_all[:].indirect(list_b[:, half // 16 :]))
+        nc.vector.tensor_scalar_min(capped[:], exp_b[:], cap[:])
+        nc.scalar.activation(log1p[:], capped[:], ACT.Ln, bias=1.0)
+
+        for n in range(2):
+            bank = score(codes_a, scales_a, 512 * n, 512, "a%d" % n, "bank%d" % (n + 2))
+            nc.vector.tensor_copy(a_all[:, 512 * n : 512 * (n + 1)], bank[:])
+        nc.vector.tensor_copy(picked_a[:, :half], a_all[:].indirect(list_a[:, : half // 16]))
+        nc.vector.tensor_tensor(softplus[:], log1p[:], picked_b[:], ALU.max)
+
+        nc.vector.scalar_tensor_tensor(squared, softplus[:], 1.0, softplus[:], ALU.add, ALU.mult)
+        inverse = sb.tile([P, I], F32, name="inverse")
+        w = sb.tile([P, I], F32, name="w")
+        nc.vector.tensor_scalar_mul(w[:, :LEAD], picked_a[:, :LEAD], lam_col[:])
+        nc.scalar.activation(inverse[:, :LEAD], squared[:, :LEAD], ACT.Abs_reciprocal_sqrt, bias=0.25)
+        nc.scalar.activation(inverse[:, LEAD:], squared[:, LEAD:], ACT.Abs_reciprocal_sqrt, bias=0.25)
+        nc.scalar.activation(picked_a[:, half:], a_all[:].indirect(list_a[:, half // 16 :]), ACT.Copy)
+        nc.vector.tensor_tensor(f1[:].indirect(list_a[:, : LEAD // 16]), w[:, :LEAD], inverse[:, :LEAD], ALU.mult)
+        nc.vector.scalar_tensor_tensor(w[:], picked_a, lam_col[:], inverse[:], ALU.mult, ALU.mult)
+        nc.vector.tensor_copy(f1[:].indirect(list_a[:, LEAD // 16 :]), w[:, LEAD:])
+
+        f2 = sb.tile([P, T], F32, name="f2")
+        nc.vector.tensor_tensor(f2[:], f1[:], old_sb[:], ALU.add)
+
+        result = sb.tile([P, I], F32, name="result")
+        picked_f = sb.tile([P, I // 2], F32, name="picked_f")
+        nc.scalar.activation(picked_f[:], f2[:].indirect(list_f[:, half // 16 :]), ACT.Copy)
+        nc.vector.tensor_tensor(result[:, :half], f2[:].indirect(list_f[:, : half // 16]), w[:, :half], ALU.mult)
+        nc.sync.dma_start(out[:, :half], result[:, :half])
+        nc.vector.tensor_tensor(result[:, half:], picked_f[:], w[:, half:], ALU.mult)
+        nc.sync.dma_start(out[:, half:], result[:, half:])

@@ -19,7 +19,6 @@ ACT = mybir.ActivationFunctionType
 P = 128
 PACK = 4
 CAP_AT = 40.0
-LEAD = 128
 
 
 def tile_attend_worthfor_lean_throughtimes_heads_kernel(
@@ -42,12 +41,12 @@ def tile_attend_worthfor_lean_throughtimes_heads_kernel(
         raw_b = sb.tile([P, PACK, Q], F32, name="raw_b", tag="raw_b_then_old")
         raw_a = sb.tile([P, PACK, Q], F32, name="raw_a")
         nc.sync.dma_start(out=raw_b[:], in_=query2.rearrange("(p j) q -> p j q", j=PACK))
-        nc.sync.dma_start(out=key_words[:].bitcast(I32), in_=keys_words[0].bitcast(I32))
         for quad in range(4):
-            nc.scalar.dma_start(
+            nc.sync.dma_start(
                 out=key_scales[32 * quad : 32 * quad + 4, :].bitcast(I32),
                 in_=keys_scales[0, 4 * quad : 4 * quad + 4, :].bitcast(I32),
             )
+        nc.sync.dma_start(out=key_words[:].bitcast(I32), in_=keys_words[0].bitcast(I32))
         nc.scalar.activation(cap[:], cap_at[:], ACT.Exp)
         nc.sync.dma_start(out=raw_a[:], in_=query.rearrange("(p j) q -> p j q", j=PACK))
         list_b = sb.tile([P, I // 16], U16, name="list_b")
@@ -106,9 +105,10 @@ def tile_attend_worthfor_lean_throughtimes_heads_kernel(
         log1p = sb.tile([P, I], F32, name="log1p")
         softplus = sb.tile([P, I], F32, name="softplus")
         half = I // 2
-        shared = sb.tile([P, I + half], F32, name="shared")
-        picked_a = shared[:, :I]
-        squared = shared[:, half:]
+        squared = sb.tile([P, I], F32, name="squared")
+        lam_wide = sb.tile([P, half], F32, name="lam_wide")
+        scaled_a = sb.tile([P, half], F32, name="scaled_a")
+        nc.vector.tensor_copy(lam_wide[:], lam_col[:].to_broadcast([P, half]))
         nc.scalar.activation(exp_b[:, half:], b_all[:].indirect(list_b[:, half // 16 :]), ACT.Exp)
         nc.vector.tensor_copy(picked_b[:, :half], b_all[:].indirect(list_b[:, : half // 16]))
         nc.scalar.activation(exp_b[:, :half], picked_b[:, :half], ACT.Exp)
@@ -119,19 +119,21 @@ def tile_attend_worthfor_lean_throughtimes_heads_kernel(
         for n in range(2):
             bank = score(codes_a, scales_a, 512 * n, 512, "a%d" % n, "bank%d" % (n + 2))
             nc.vector.tensor_copy(a_all[:, 512 * n : 512 * (n + 1)], bank[:])
-        nc.vector.tensor_copy(picked_a[:, :half], a_all[:].indirect(list_a[:, : half // 16]))
+        nc.vector.tensor_tensor(scaled_a[:], a_all[:].indirect(list_a[:, : half // 16]), lam_wide[:], ALU.mult)
         nc.vector.tensor_tensor(softplus[:], log1p[:], picked_b[:], ALU.max)
 
-        nc.vector.scalar_tensor_tensor(squared, softplus[:], 1.0, softplus[:], ALU.add, ALU.mult)
+        nc.vector.scalar_tensor_tensor(squared[:], softplus[:], 1.0, softplus[:], ALU.add, ALU.mult)
         inverse = sb.tile([P, I], F32, name="inverse")
-        w = sb.tile([P, I], F32, name="w")
-        nc.vector.tensor_scalar_mul(w[:, :LEAD], picked_a[:, :LEAD], lam_col[:])
-        nc.scalar.activation(inverse[:, :LEAD], squared[:, :LEAD], ACT.Abs_reciprocal_sqrt, bias=0.25)
-        nc.scalar.activation(inverse[:, LEAD:], squared[:, LEAD:], ACT.Abs_reciprocal_sqrt, bias=0.25)
-        nc.scalar.activation(picked_a[:, half:], a_all[:].indirect(list_a[:, half // 16 :]), ACT.Copy)
-        nc.vector.tensor_tensor(f1[:].indirect(list_a[:, : LEAD // 16]), w[:, :LEAD], inverse[:, :LEAD], ALU.mult)
-        nc.vector.scalar_tensor_tensor(w[:], picked_a, lam_col[:], inverse[:], ALU.mult, ALU.mult)
-        nc.vector.tensor_copy(f1[:].indirect(list_a[:, LEAD // 16 :]), w[:, LEAD:])
+        w_hi = sb.tile([P, half], F32, name="w_hi")
+        nc.scalar.activation(inverse[:, :half], squared[:, :half], ACT.Abs_reciprocal_sqrt, bias=0.25)
+        nc.scalar.activation(inverse[:, half:], squared[:, half:], ACT.Abs_reciprocal_sqrt, bias=0.25)
+        picked_a = squared[:, half:]
+        nc.scalar.activation(picked_a, a_all[:].indirect(list_a[:, half // 16 :]), ACT.Copy)
+        nc.vector.tensor_tensor(f1[:].indirect(list_a[:, : half // 16]), scaled_a[:], inverse[:, :half], ALU.mult)
+        nc.vector.scalar_tensor_tensor(w_hi[:], picked_a, lam_col[:], inverse[:, half:], ALU.mult, ALU.mult)
+        nc.vector.tensor_copy(f1[:].indirect(list_a[:, half // 16 :]), w_hi[:])
+        w_lo = squared[:, half:]
+        nc.vector.tensor_tensor(w_lo, scaled_a[:], inverse[:, :half], ALU.mult)
 
         f2 = sb.tile([P, T], F32, name="f2")
         nc.vector.tensor_tensor(f2[:], f1[:], old_sb[:], ALU.add)
@@ -139,7 +141,7 @@ def tile_attend_worthfor_lean_throughtimes_heads_kernel(
         result = sb.tile([P, I], F32, name="result")
         picked_f = sb.tile([P, I // 2], F32, name="picked_f")
         nc.scalar.activation(picked_f[:], f2[:].indirect(list_f[:, half // 16 :]), ACT.Copy)
-        nc.vector.tensor_tensor(result[:, :half], f2[:].indirect(list_f[:, : half // 16]), w[:, :half], ALU.mult)
+        nc.vector.tensor_tensor(result[:, :half], f2[:].indirect(list_f[:, : half // 16]), w_lo, ALU.mult)
         nc.sync.dma_start(out[:, :half], result[:, :half])
-        nc.vector.tensor_tensor(result[:, half:], picked_f[:], w[:, half:], ALU.mult)
+        nc.vector.tensor_tensor(result[:, half:], picked_f[:], w_hi[:], ALU.mult)
         nc.sync.dma_start(out[:, half:], result[:, half:])

@@ -19,6 +19,7 @@ ACT = mybir.ActivationFunctionType
 P = 128
 PACK = 4
 CAP_AT = 40.0
+B_CUTS = (0, 256, 512, 768, 896, 1024)
 
 
 def tile_attend_worthfor_lean_throughtimes_heads_kernel(
@@ -30,25 +31,27 @@ def tile_attend_worthfor_lean_throughtimes_heads_kernel(
         ps = ctx.enter_context(tc.psum_pool(name="ps", bufs=1))
 
         key_scales = sb.tile([P, T], U8, name="key_scales", align_bytes=64)
-        key_words = sb.tile([P, 2 * T], U8, name="key_words", align_bytes=64)
+        key_words = [sb.tile([P, T], U8, name="key_words%d" % h, align_bytes=64) for h in range(2)]
         f1 = sb.tile([P, T], F32, name="f1")
-        nc.gpsimd.memset(key_scales[:].bitcast(I32), 0)
-        nc.vector.memset(f1[:], 0.0)
+        nc.vector.memset(key_scales[:].bitcast(I32), 0)
 
         cap_at = sb.tile([P, 1], F32, name="cap_at")
         cap = sb.tile([P, 1], F32, name="cap")
         nc.vector.memset(cap_at[:], CAP_AT)
+        nc.vector.memset(f1[:], 0.0)
         raw_b = sb.tile([P, PACK, Q], F32, name="raw_b", tag="raw_b_then_old")
         raw_a = sb.tile([P, PACK, Q], F32, name="raw_a")
         nc.sync.dma_start(out=raw_b[:], in_=query2.rearrange("(p j) q -> p j q", j=PACK))
         for quad in range(4):
-            nc.sync.dma_start(
+            queue = nc.sync if quad == 0 else nc.scalar
+            queue.dma_start(
                 out=key_scales[32 * quad : 32 * quad + 4, :].bitcast(I32),
                 in_=keys_scales[0, 4 * quad : 4 * quad + 4, :].bitcast(I32),
             )
-        nc.sync.dma_start(out=key_words[:].bitcast(I32), in_=keys_words[0].bitcast(I32))
+        nc.sync.dma_start(out=key_words[0][:].bitcast(I32), in_=keys_words[0, :, :T].bitcast(I32))
         nc.scalar.activation(cap[:], cap_at[:], ACT.Exp)
         nc.sync.dma_start(out=raw_a[:], in_=query.rearrange("(p j) q -> p j q", j=PACK))
+        nc.sync.dma_start(out=key_words[1][:].bitcast(I32), in_=keys_words[0, :, T:].bitcast(I32))
         list_b = sb.tile([P, I // 16], U16, name="list_b")
         list_a = sb.tile([P, I // 16], U16, name="list_a")
         list_f = sb.tile([P, I // 16], U16, name="list_f")
@@ -59,7 +62,7 @@ def tile_attend_worthfor_lean_throughtimes_heads_kernel(
         nc.sync.dma_start(lam_col[:], lam)
 
         def quantise(raw, tag):
-            grouped = sb.tile([P, Q, PACK], BF16, name=tag + "_grouped", align_bytes=64)
+            grouped = sb.tile([P, Q, PACK], BF16, name=tag + "_grouped", tag="grouped", align_bytes=64)
             codes = sb.tile([P, Q], U32, name=tag + "_codes", align_bytes=64)
             scales = sb.tile([P, Q], U8, name=tag + "_scales", align_bytes=64)
             nc.vector.tensor_copy(
@@ -79,7 +82,7 @@ def tile_attend_worthfor_lean_throughtimes_heads_kernel(
                 out=bank[:],
                 lhsT=codes[:].bitcast(FP8X4),
                 lhsT_scale=scales[:],
-                rhs=key_words[:, 2 * first : 2 * (first + width)].bitcast(FP4X4),
+                rhs=key_words[first // 512][:, 2 * (first % 512) : 2 * (first % 512 + width)].bitcast(FP4X4),
                 rhs_scale=key_scales[:, first : first + width],
                 start=True,
                 stop=True,
@@ -89,15 +92,15 @@ def tile_attend_worthfor_lean_throughtimes_heads_kernel(
         b_all = sb.tile([P, T], F32, name="b_all")
         a_all = sb.tile([P, T], F32, name="a_all")
         codes_b, scales_b = quantise(raw_b, "b")
+        codes_a, scales_a = quantise(raw_a, "a")
         old_sb = sb.tile([P, T], F32, name="old_sb", tag="raw_b_then_old")
         nc.sync.dma_start(old_sb[:], old)
-        for n in range(4):
-            bank = score(codes_b, scales_b, 256 * n, 256, "b%d" % n, "bank%d" % n)
+        for n, (lo, hi) in enumerate(zip(B_CUTS, B_CUTS[1:])):
+            bank = score(codes_b, scales_b, lo, hi - lo, "b%d" % n, "bank%d" % n)
             if n % 2 == 0:
-                nc.scalar.activation(b_all[:, 256 * n : 256 * (n + 1)], bank[:], ACT.Copy)
+                nc.scalar.activation(b_all[:, lo:hi], bank[:], ACT.Copy)
             else:
-                nc.vector.tensor_copy(b_all[:, 256 * n : 256 * (n + 1)], bank[:])
-        codes_a, scales_a = quantise(raw_a, "a")
+                nc.vector.tensor_copy(b_all[:, lo:hi], bank[:])
 
         exp_b = sb.tile([P, I], F32, name="exp_b")
         picked_b = sb.tile([P, I], F32, name="picked_b")
@@ -106,9 +109,8 @@ def tile_attend_worthfor_lean_throughtimes_heads_kernel(
         softplus = sb.tile([P, I], F32, name="softplus")
         half = I // 2
         squared = sb.tile([P, I], F32, name="squared")
-        lam_wide = sb.tile([P, half], F32, name="lam_wide")
+        picked_lo = sb.tile([P, half], F32, name="picked_lo")
         scaled_a = sb.tile([P, half], F32, name="scaled_a")
-        nc.vector.tensor_copy(lam_wide[:], lam_col[:].to_broadcast([P, half]))
         nc.scalar.activation(exp_b[:, half:], b_all[:].indirect(list_b[:, half // 16 :]), ACT.Exp)
         nc.vector.tensor_copy(picked_b[:, :half], b_all[:].indirect(list_b[:, : half // 16]))
         nc.scalar.activation(exp_b[:, :half], picked_b[:, :half], ACT.Exp)
@@ -117,12 +119,17 @@ def tile_attend_worthfor_lean_throughtimes_heads_kernel(
         nc.scalar.activation(log1p[:], capped[:], ACT.Ln, bias=1.0)
 
         for n in range(2):
-            bank = score(codes_a, scales_a, 512 * n, 512, "a%d" % n, "bank%d" % (n + 2))
+            bank = score(codes_a, scales_a, 512 * n, 512, "a%d" % n, "bank%d" % (n + 3))
             nc.vector.tensor_copy(a_all[:, 512 * n : 512 * (n + 1)], bank[:])
-        nc.vector.tensor_tensor(scaled_a[:], a_all[:].indirect(list_a[:, : half // 16]), lam_wide[:], ALU.mult)
-        nc.vector.tensor_tensor(softplus[:], log1p[:], picked_b[:], ALU.max)
-
-        nc.vector.scalar_tensor_tensor(squared[:], softplus[:], 1.0, softplus[:], ALU.add, ALU.mult)
+        nc.vector.tensor_copy(picked_lo[:], a_all[:].indirect(list_a[:, : half // 16]))
+        halves = (slice(0, half), slice(half, I))
+        for part in halves:
+            nc.vector.tensor_tensor(softplus[:, part], log1p[:, part], picked_b[:, part], ALU.max)
+        for part in halves:
+            nc.vector.scalar_tensor_tensor(
+                squared[:, part], softplus[:, part], 1.0, softplus[:, part], ALU.add, ALU.mult
+            )
+        nc.vector.tensor_scalar_mul(scaled_a[:], picked_lo[:], lam_col[:])
         inverse = sb.tile([P, I], F32, name="inverse")
         w_hi = sb.tile([P, half], F32, name="w_hi")
         nc.scalar.activation(inverse[:, :half], squared[:, :half], ACT.Abs_reciprocal_sqrt, bias=0.25)
@@ -133,7 +140,8 @@ def tile_attend_worthfor_lean_throughtimes_heads_kernel(
         nc.vector.scalar_tensor_tensor(w_hi[:], picked_a, lam_col[:], inverse[:, half:], ALU.mult, ALU.mult)
         nc.vector.tensor_copy(f1[:].indirect(list_a[:, half // 16 :]), w_hi[:])
         w_lo = squared[:, half:]
-        nc.vector.tensor_tensor(w_lo, scaled_a[:], inverse[:, :half], ALU.mult)
+        for part in (slice(0, half // 2), slice(half // 2, half)):
+            nc.vector.tensor_tensor(w_lo[:, part], scaled_a[:, part], inverse[:, part], ALU.mult)
 
         f2 = sb.tile([P, T], F32, name="f2")
         nc.vector.tensor_tensor(f2[:], f1[:], old_sb[:], ALU.add)

@@ -42,13 +42,12 @@ def tile_attend_worthfor_lean_throughtimes_heads_kernel(
         raw_b = sb.tile([P, PACK, Q], F32, name="raw_b", tag="raw_b_then_old")
         raw_a = sb.tile([P, PACK, Q], F32, name="raw_a")
         nc.sync.dma_start(out=raw_b[:], in_=query2.rearrange("(p j) q -> p j q", j=PACK))
+        nc.sync.dma_start(out=key_words[0][:].bitcast(I32), in_=keys_words[0, :, :T].bitcast(I32))
         for quad in range(4):
-            queue = nc.sync if quad == 0 else nc.scalar
-            queue.dma_start(
+            nc.sync.dma_start(
                 out=key_scales[32 * quad : 32 * quad + 4, :].bitcast(I32),
                 in_=keys_scales[0, 4 * quad : 4 * quad + 4, :].bitcast(I32),
             )
-        nc.sync.dma_start(out=key_words[0][:].bitcast(I32), in_=keys_words[0, :, :T].bitcast(I32))
         nc.scalar.activation(cap[:], cap_at[:], ACT.Exp)
         nc.sync.dma_start(out=raw_a[:], in_=query.rearrange("(p j) q -> p j q", j=PACK))
         nc.sync.dma_start(out=key_words[1][:].bitcast(I32), in_=keys_words[0, :, T:].bitcast(I32))

@@ -146,9 +146,11 @@ def tile_attend_worthfor_lean_throughtimes_heads_kernel(
         nc.vector.tensor_tensor(f2[:], f1[:], old_sb[:], ALU.add)
 
         result = sb.tile([P, I], F32, name="result")
-        picked_f = sb.tile([P, I // 2], F32, name="picked_f")
-        nc.scalar.activation(picked_f[:], f2[:].indirect(list_f[:, half // 16 :]), ACT.Copy)
-        nc.vector.tensor_tensor(result[:, :half], f2[:].indirect(list_f[:, : half // 16]), w_lo, ALU.mult)
-        nc.sync.dma_start(out[:, :half], result[:, :half])
-        nc.vector.tensor_tensor(result[:, half:], picked_f[:], w_hi[:], ALU.mult)
-        nc.sync.dma_start(out[:, half:], result[:, half:])
+        quarter = half // 2
+        for lo, hi, weights in (
+            (0, half, w_lo),
+            (half, half + quarter, w_hi[:, :quarter]),
+            (half + quarter, I, w_hi[:, quarter:]),
+        ):
+            nc.vector.tensor_tensor(result[:, lo:hi], f2[:].indirect(list_f[:, lo // 16 : hi // 16]), weights, ALU.mult)
+            nc.sync.dma_start(out[:, lo:hi], result[:, lo:hi])

from contextlib import ExitStack

import concourse.mybir as mybir

D, T, I, Q = 512, 1024, 512, 128
FLOPS = 2 * 2 * D * T * Q

F32 = mybir.dt.float32
BF16 = mybir.dt.bfloat16
I32 = mybir.dt.int32
U32 = mybir.dt.uint32
U16 = mybir.dt.uint16
U8 = mybir.dt.uint8
FP8X4 = mybir.dt.float8_e4m3fn_x4
FP4X4 = mybir.dt.float4_e2m1fn_x4
ALU = mybir.AluOpType
ACT = mybir.ActivationFunctionType

P = 128
PACK = 4
CAP_AT = 40.0
B_CUTS = (0, 256, 512, 768, 896, 1024)


def tile_attend_worthfor_lean_throughtimes_heads_kernel(
    tc, query, query2, keys_words, keys_scales, lam, old, offs, offs2, offs3, out
):
    nc = tc.nc
    with ExitStack() as ctx:
        sb = ctx.enter_context(tc.tile_pool(name="sb", bufs=1))
        ps = ctx.enter_context(tc.psum_pool(name="ps", bufs=1))

        key_scales = sb.tile([P, T], U8, name="key_scales", align_bytes=64)
        key_words = [sb.tile([P, T], U8, name="key_words%d" % h, align_bytes=64) for h in range(2)]
        f1 = sb.tile([P, T], F32, name="f1")
        nc.vector.memset(key_scales[:].bitcast(I32), 0)

        cap_at = sb.tile([P, 1], F32, name="cap_at")
        cap = sb.tile([P, 1], F32, name="cap")
        nc.vector.memset(cap_at[:], CAP_AT)
        nc.vector.memset(f1[:], 0.0)
        raw_b = sb.tile([P, PACK, Q], F32, name="raw_b", tag="raw_b_then_old")
        raw_a = sb.tile([P, PACK, Q], F32, name="raw_a")
        nc.sync.dma_start(out=raw_b[:], in_=query2.rearrange("(p j) q -> p j q", j=PACK))
        nc.sync.dma_start(out=key_words[0][:].bitcast(I32), in_=keys_words[0, :, :T].bitcast(I32))
        for quad in range(4):
            nc.sync.dma_start(
                out=key_scales[32 * quad : 32 * quad + 4, :].bitcast(I32),
                in_=keys_scales[0, 4 * quad : 4 * quad + 4, :].bitcast(I32),
            )
        nc.scalar.activation(cap[:], cap_at[:], ACT.Exp)
        nc.sync.dma_start(out=raw_a[:], in_=query.rearrange("(p j) q -> p j q", j=PACK))
        nc.sync.dma_start(out=key_words[1][:].bitcast(I32), in_=keys_words[0, :, T:].bitcast(I32))
        list_b = sb.tile([P, I // 16], U16, name="list_b")
        list_a = sb.tile([P, I // 16], U16, name="list_a")
        list_f = sb.tile([P, I // 16], U16, name="list_f")
        lam_col = sb.tile([P, 1], F32, name="lam_col")
        nc.sync.dma_start(list_b[:], offs2)
        nc.sync.dma_start(list_a[:], offs)
        nc.sync.dma_start(list_f[:], offs3)
        nc.sync.dma_start(lam_col[:], lam)

        def quantise(raw, tag):
            grouped = sb.tile([P, Q, PACK], BF16, name=tag + "_grouped", tag="grouped", align_bytes=64)
            codes = sb.tile([P, Q], U32, name=tag + "_codes", align_bytes=64)
            scales = sb.tile([P, Q], U8, name=tag + "_scales", align_bytes=64)
            nc.vector.tensor_copy(
                out=grouped[:].rearrange("p (c i) j -> p c j i", i=4),
                in_=raw[:].rearrange("p j (c i) -> p c j i", i=4),
            )
            nc.vector.quantize_mx(
                out=codes[:].bitcast(FP8X4),
                scales=scales[:],
                in_=grouped[:].rearrange("p q j -> p (q j)"),
            )
            return codes, scales

        def score(codes, scales, first, width, name, tag):
            bank = ps.tile([P, width], F32, name=name, tag=tag)
            nc.tensor.matmul_mx(
                out=bank[:],
                lhsT=codes[:].bitcast(FP8X4),
                lhsT_scale=scales[:],
                rhs=key_words[first // 512][:, 2 * (first % 512) : 2 * (first % 512 + width)].bitcast(FP4X4),
                rhs_scale=key_scales[:, first : first + width],
                start=True,
                stop=True,
            )
            return bank

        b_all = sb.tile([P, T], F32, name="b_all")
        a_all = sb.tile([P, T], F32, name="a_all")
        codes_b, scales_b = quantise(raw_b, "b")
        codes_a, scales_a = quantise(raw_a, "a")
        old_sb = sb.tile([P, T], F32, name="old_sb", tag="raw_b_then_old")
        nc.sync.dma_start(old_sb[:], old)
        for n, (lo, hi) in enumerate(zip(B_CUTS, B_CUTS[1:])):
            bank = score(codes_b, scales_b, lo, hi - lo, "b%d" % n, "bank%d" % n)
            if n % 2 == 0:
                nc.scalar.activation(b_all[:, lo:hi], bank[:], ACT.Copy)
            else:
                nc.vector.tensor_copy(b_all[:, lo:hi], bank[:])

        exp_b = sb.tile([P, I], F32, name="exp_b")
        picked_b = sb.tile([P, I], F32, name="picked_b")
        capped = sb.tile([P, I], F32, name="capped")
        log1p = sb.tile([P, I], F32, name="log1p")
        softplus = sb.tile([P, I], F32, name="softplus")
        half = I // 2
        squared = sb.tile([P, I], F32, name="squared")
        picked_lo = sb.tile([P, half], F32, name="picked_lo")
        scaled_a = sb.tile([P, half], F32, name="scaled_a")
        nc.scalar.activation(exp_b[:, half:], b_all[:].indirect(list_b[:, half // 16 :]), ACT.Exp)
        nc.vector.tensor_copy(picked_b[:, :half], b_all[:].indirect(list_b[:, : half // 16]))
        nc.scalar.activation(exp_b[:, :half], picked_b[:, :half], ACT.Exp)
        nc.vector.tensor_copy(picked_b[:, half:], b_all[:].indirect(list_b[:, half // 16 :]))
        nc.vector.tensor_scalar_min(capped[:], exp_b[:], cap[:])
        nc.scalar.activation(log1p[:], capped[:], ACT.Ln, bias=1.0)

        for n in range(2):
            bank = score(codes_a, scales_a, 512 * n, 512, "a%d" % n, "bank%d" % (n + 3))
            nc.vector.tensor_copy(a_all[:, 512 * n : 512 * (n + 1)], bank[:])
        nc.vector.tensor_copy(picked_lo[:], a_all[:].indirect(list_a[:, : half // 16]))
        halves = (slice(0, half), slice(half, I))
        for part in halves:
            nc.vector.tensor_tensor(softplus[:, part], log1p[:, part], picked_b[:, part], ALU.max)
        for part in halves:
            nc.vector.scalar_tensor_tensor(
                squared[:, part], softplus[:, part], 1.0, softplus[:, part], ALU.add, ALU.mult
            )
        nc.vector.tensor_scalar_mul(scaled_a[:], picked_lo[:], lam_col[:])
        inverse = sb.tile([P, I], F32, name="inverse")
        w_hi = sb.tile([P, half], F32, name="w_hi")
        nc.scalar.activation(inverse[:, :half], squared[:, :half], ACT.Abs_reciprocal_sqrt, bias=0.25)
        nc.scalar.activation(inverse[:, half:], squared[:, half:], ACT.Abs_reciprocal_sqrt, bias=0.25)
        picked_a = squared[:, half:]
        nc.scalar.activation(picked_a, a_all[:].indirect(list_a[:, half // 16 :]), ACT.Copy)
        nc.vector.tensor_tensor(f1[:].indirect(list_a[:, : half // 16]), scaled_a[:], inverse[:, :half], ALU.mult)
        nc.vector.scalar_tensor_tensor(w_hi[:], picked_a, lam_col[:], inverse[:, half:], ALU.mult, ALU.mult)
        nc.vector.tensor_copy(f1[:].indirect(list_a[:, half // 16 :]), w_hi[:])
        w_lo = squared[:, half:]
        for part in (slice(0, half // 2), slice(half // 2, half)):
            nc.vector.tensor_tensor(w_lo[:, part], scaled_a[:, part], inverse[:, part], ALU.mult)

        f2 = sb.tile([P, T], F32, name="f2")
        nc.vector.tensor_tensor(f2[:], f1[:], old_sb[:], ALU.add)

        result = sb.tile([P, I], F32, name="result")
        quarter = half // 2
        for lo, hi, weights in (
            (0, half, w_lo),
            (half, half + quarter, w_hi[:, :quarter]),
            (half + quarter, I, w_hi[:, quarter:]),
        ):
            nc.vector.tensor_tensor(result[:, lo:hi], f2[:].indirect(list_f[:, lo // 16 : hi // 16]), weights, ALU.mult)
            nc.sync.dma_start(out[:, lo:hi], result[:, lo:hi])
